import numpy as np
import ml_dtypes

BF16 = ml_dtypes.bfloat16


def bf(x):
    return np.asarray(x, np.float32).astype(BF16)


def f32(x):
    return np.asarray(x, np.float32)


def f64(x):
    return np.asarray(x).astype(np.float64)


def striped(idx):
    return np.tile(idx.reshape(-1, 16).T, (8, 1))


S, K, M, N, B, Q = 512, 512, 128, 256, 2, 128


def setup_inputs():
    return {"base": bf(np.random.standard_normal((B, M, S))), "x": bf(np.random.standard_normal((K, N))), "w": bf(np.random.standard_normal((K, M)) / np.sqrt(K)), "b": f32(0.5 * np.random.standard_normal((M, 1))), "offs": striped(np.random.permutation(S)[:N])}


def reference(base, x, w, b, offs):
    idx = offs[:16].T.reshape(-1)
    z = f64(base).copy()
    for i in range(B):
        z[i][:, idx[i * Q : (i + 1) * Q]] += f64(w).T @ f64(x)[:, i * Q : (i + 1) * Q]
    return z + f64(b)

@@ -1,0 +1,61 @@
+import concourse.mybir as mybir
+from concourse.masks import make_identity
+
+BF16, F32, U16 = mybir.dt.bfloat16, mybir.dt.float32, mybir.dt.uint16
+
+P = 128
+SEQS = 2
+TOKENS = 512
+K = 512
+KBLOCKS = K // P
+N = 256
+PIECE = N // SEQS
+PIECE_COLS = PIECE // 16
+
+FLOPS = 2 * K * P * N
+
+
+def tile_scatter_matmul_kernel(tc, base, x, w, b, offs, out):
+    nc = tc.nc
+    with (
+        tc.tile_pool(name="held", bufs=1) as held,
+        tc.psum_pool(name="windows", bufs=1) as windows,
+    ):
+        offsets = held.tile([P, N // 16], U16, name="offsets")
+        nc.sync.dma_start(offsets[:], offs)
+
+        base_tiles = [held.tile([P, TOKENS], BF16, name="base%d" % i) for i in range(SEQS)]
+        nc.sync.dma_start(base_tiles[0][:], base[0])
+        nc.scalar.dma_start(base_tiles[1][:], base[1])
+
+        w_tile = held.tile([P, KBLOCKS, P], BF16, name="w_tile")
+        nc.sync.dma_start(w_tile[:], w.rearrange("(a p) m -> p a m", p=P))
+        x_tile = held.tile([P, KBLOCKS, N], BF16, name="x_tile")
+        nc.scalar.dma_start(x_tile[:], x.rearrange("(a p) n -> p a n", p=P))
+
+        ident = held.tile([P, P], BF16, name="ident")
+        make_identity(nc, ident[:])
+
+        bias = held.tile([P, 1], F32, name="bias")
+        nc.gpsimd.dma_start(bias[:], b)
+
+        window_tiles = [windows.tile([P, TOKENS], F32, name="window%d" % i) for i in range(SEQS)]
+        for i in range(SEQS):
+            nc.tensor.matmul(window_tiles[i][:], ident[:], base_tiles[i][:], start=True, stop=False)
+
+        for i in range(SEQS):
+            piece = offsets[:, i * PIECE_COLS : (i + 1) * PIECE_COLS]
+            for a in range(KBLOCKS):
+                nc.tensor.matmul(
+                    window_tiles[i][:].indirect(piece),
+                    w_tile[:, a, :],
+                    x_tile[:, a, i * PIECE : (i + 1) * PIECE],
+                    start=False,
+                    stop=(a == KBLOCKS - 1),
+                )
+
+        store_queues = [nc.sync, nc.scalar]
+        for i in range(SEQS):
+            result = held.tile([P, TOKENS], F32, name="result%d" % i)
+            nc.vector.tensor_scalar_add(result[:], window_tiles[i][:], bias[:, 0:1])
+            store_queues[i].dma_start(out[i], result[:])

@@ -12,6 +12,8 @@ N = 256
 PIECE = N // SEQS
 PIECE_COLS = PIECE // 16
 
+WARMUP = 16
+
 FLOPS = 2 * K * P * N
 
 
@@ -37,7 +39,13 @@ def tile_scatter_matmul_kernel(tc, base, x, w, b, offs, out):
         make_identity(nc, ident[:])
 
         bias = held.tile([P, 1], F32, name="bias")
-        nc.gpsimd.dma_start(bias[:], b)
+        nc.scalar.dma_start(bias[:], b)
+
+        zeros = held.tile([P, P], BF16, name="zeros")
+        nc.vector.memset(zeros[:], 0.0)
+        spare = windows.tile([P, P], F32, name="spare")
+        for r in range(WARMUP):
+            nc.tensor.matmul(spare[:], zeros[:], zeros[:], start=True, stop=True)
 
         window_tiles = [windows.tile([P, TOKENS], F32, name="window%d" % i) for i in range(SEQS)]
         for i in range(SEQS):

@@ -23,17 +23,17 @@ def tile_scatter_matmul_kernel(tc, base, x, w, b, offs, out):
         tc.tile_pool(name="held", bufs=1) as held,
         tc.psum_pool(name="windows", bufs=1) as windows,
     ):
-        offsets = held.tile([P, N // 16], U16, name="offsets")
-        nc.sync.dma_start(offsets[:], offs)
-
         base_tiles = [held.tile([P, TOKENS], BF16, name="base%d" % i) for i in range(SEQS)]
         nc.sync.dma_start(base_tiles[0][:], base[0])
         nc.scalar.dma_start(base_tiles[1][:], base[1])
 
+        offsets = held.tile([P, N // 16], U16, name="offsets")
+        nc.sync.dma_start(offsets[:], offs)
+
         w_tile = held.tile([P, KBLOCKS, P], BF16, name="w_tile")
-        nc.sync.dma_start(w_tile[:], w.rearrange("(a p) m -> p a m", p=P))
+        nc.sync.dma_start(w_tile[:], w.rearrange("(p a) m -> p a m", a=KBLOCKS))
         x_tile = held.tile([P, KBLOCKS, N], BF16, name="x_tile")
-        nc.scalar.dma_start(x_tile[:], x.rearrange("(a p) n -> p a n", p=P))
+        nc.scalar.dma_start(x_tile[:], x.rearrange("(p a) n -> p a n", a=KBLOCKS))
 
         ident = held.tile([P, P], BF16, name="ident")
         make_identity(nc, ident[:])

@@ -6,6 +6,7 @@ BF16, F32, U16 = mybir.dt.bfloat16, mybir.dt.float32, mybir.dt.uint16
 P = 128
 SEQS = 2
 TOKENS = 512
+HALF = TOKENS // 2
 K = 512
 KBLOCKS = K // P
 N = 256
@@ -64,6 +65,8 @@ def tile_scatter_matmul_kernel(tc, base, x, w, b, offs, out):
 
         store_queues = [nc.sync, nc.scalar]
         for i in range(SEQS):
-            result = held.tile([P, TOKENS], F32, name="result%d" % i)
-            nc.vector.tensor_scalar_add(result[:], window_tiles[i][:], bias[:, 0:1])
-            store_queues[i].dma_start(out[i], result[:])
+            for h in range(2):
+                columns = slice(h * HALF, (h + 1) * HALF)
+                result = held.tile([P, HALF], F32, name="result%d_%d" % (i, h))
+                nc.vector.tensor_scalar_add(result[:], window_tiles[i][:, columns], bias[:, 0:1])
+                store_queues[h].dma_start(out[i][:, columns], result[:])

@@ -6,14 +6,13 @@ BF16, F32, U16 = mybir.dt.bfloat16, mybir.dt.float32, mybir.dt.uint16
 P = 128
 SEQS = 2
 TOKENS = 512
-HALF = TOKENS // 2
 K = 512
 KBLOCKS = K // P
 N = 256
 PIECE = N // SEQS
 PIECE_COLS = PIECE // 16
 
-WARMUP = 16
+WARMUP = 12
 
 FLOPS = 2 * K * P * N
 
@@ -65,8 +64,6 @@ def tile_scatter_matmul_kernel(tc, base, x, w, b, offs, out):
 
         store_queues = [nc.sync, nc.scalar]
         for i in range(SEQS):
-            for h in range(2):
-                columns = slice(h * HALF, (h + 1) * HALF)
-                result = held.tile([P, HALF], F32, name="result%d_%d" % (i, h))
-                nc.vector.tensor_scalar_add(result[:], window_tiles[i][:, columns], bias[:, 0:1])
-                store_queues[h].dma_start(out[i][:, columns], result[:])
+            result = held.tile([P, TOKENS], F32, name="result%d" % i)
+            nc.vector.tensor_scalar_add(result[:], window_tiles[i][:], bias[:, 0:1])
+            store_queues[i].dma_start(out[i], result[:])

@@ -2,6 +2,7 @@ import concourse.mybir as mybir
 from concourse.masks import make_identity
 
 BF16, F32, U16 = mybir.dt.bfloat16, mybir.dt.float32, mybir.dt.uint16
+IDENTITY = mybir.ActivationFunctionType.Identity
 
 P = 128
 SEQS = 2
@@ -41,6 +42,11 @@ def tile_scatter_matmul_kernel(tc, base, x, w, b, offs, out):
         bias = held.tile([P, 1], F32, name="bias")
         nc.scalar.dma_start(bias[:], b)
 
+        zero_column = held.tile([P, 1], F32, name="zero_column")
+        nc.vector.memset(zero_column[:], 0.0)
+        unused_column = held.tile([P, 1], F32, name="unused_column")
+        nc.scalar.activation(unused_column[:], zero_column[:], IDENTITY)
+
         zeros = held.tile([P, P], BF16, name="zeros")
         nc.vector.memset(zeros[:], 0.0)
         spare = windows.tile([P, P], F32, name="spare")
@@ -62,8 +68,8 @@ def tile_scatter_matmul_kernel(tc, base, x, w, b, offs, out):
                     stop=(a == KBLOCKS - 1),
                 )
 
-        store_queues = [nc.sync, nc.scalar]
-        for i in range(SEQS):
-            result = held.tile([P, TOKENS], F32, name="result%d" % i)
-            nc.vector.tensor_scalar_add(result[:], window_tiles[i][:], bias[:, 0:1])
-            store_queues[i].dma_start(out[i], result[:])
+        result_tiles = [held.tile([P, TOKENS], F32, name="result%d" % i) for i in range(SEQS)]
+        nc.scalar.activation(result_tiles[0][:], window_tiles[0][:], IDENTITY, bias=bias[:, 0:1])
+        nc.scalar.dma_start(out[0], result_tiles[0][:])
+        nc.vector.tensor_scalar_add(result_tiles[1][:], window_tiles[1][:], bias[:, 0:1])
+        nc.sync.dma_start(out[1], result_tiles[1][:])

@@ -7,6 +7,7 @@ IDENTITY = mybir.ActivationFunctionType.Identity
 P = 128
 SEQS = 2
 TOKENS = 512
+HALF = TOKENS // 2
 K = 512
 KBLOCKS = K // P
 N = 256
@@ -68,8 +69,16 @@ def tile_scatter_matmul_kernel(tc, base, x, w, b, offs, out):
                     stop=(a == KBLOCKS - 1),
                 )
 
-        result_tiles = [held.tile([P, TOKENS], F32, name="result%d" % i) for i in range(SEQS)]
-        nc.scalar.activation(result_tiles[0][:], window_tiles[0][:], IDENTITY, bias=bias[:, 0:1])
-        nc.scalar.dma_start(out[0], result_tiles[0][:])
-        nc.vector.tensor_scalar_add(result_tiles[1][:], window_tiles[1][:], bias[:, 0:1])
-        nc.sync.dma_start(out[1], result_tiles[1][:])
+        halves = [slice(h * HALF, (h + 1) * HALF) for h in range(2)]
+        result_tiles = [
+            [held.tile([P, HALF], F32, name="result%d_%d" % (i, h)) for h in range(2)] for i in range(SEQS)
+        ]
+        for h in range(2):
+            nc.scalar.activation(
+                result_tiles[0][h][:], window_tiles[0][:, halves[h]], IDENTITY, bias=bias[:, 0:1]
+            )
+        nc.sync.dma_start(out[0][:, halves[0]], result_tiles[0][0][:])
+        nc.scalar.dma_start(out[0][:, halves[1]], result_tiles[0][1][:])
+        for h in range(2):
+            nc.vector.tensor_scalar_add(result_tiles[1][h][:], window_tiles[1][:, halves[h]], bias[:, 0:1])
+            nc.sync.dma_start(out[1][:, halves[h]], result_tiles[1][h][:])

@@ -25,23 +25,22 @@ def tile_scatter_matmul_kernel(tc, base, x, w, b, offs, out):
         tc.tile_pool(name="held", bufs=1) as held,
         tc.psum_pool(name="windows", bufs=1) as windows,
     ):
-        base_tiles = [held.tile([P, TOKENS], BF16, name="base%d" % i) for i in range(SEQS)]
-        nc.sync.dma_start(base_tiles[0][:], base[0])
-        nc.scalar.dma_start(base_tiles[1][:], base[1])
+        base_tile = held.tile([P, SEQS, TOKENS], BF16, name="base_tile")
+        nc.sync.dma_start(base_tile[:], base.rearrange("i m t -> m i t"))
 
         offsets = held.tile([P, N // 16], U16, name="offsets")
         nc.sync.dma_start(offsets[:], offs)
 
         w_tile = held.tile([P, KBLOCKS, P], BF16, name="w_tile")
-        nc.sync.dma_start(w_tile[:], w.rearrange("(p a) m -> p a m", a=KBLOCKS))
+        nc.scalar.dma_start(w_tile[:], w.rearrange("(p a) m -> p a m", a=KBLOCKS))
         x_tile = held.tile([P, KBLOCKS, N], BF16, name="x_tile")
-        nc.scalar.dma_start(x_tile[:], x.rearrange("(p a) n -> p a n", a=KBLOCKS))
+        nc.sync.dma_start(x_tile[:], x.rearrange("(p a) n -> p a n", a=KBLOCKS))
+
+        bias = held.tile([P, 1], F32, name="bias")
+        nc.gpsimd.dma_start(bias[:], b)
 
         ident = held.tile([P, P], BF16, name="ident")
         make_identity(nc, ident[:])
-
-        bias = held.tile([P, 1], F32, name="bias")
-        nc.scalar.dma_start(bias[:], b)
 
         zero_column = held.tile([P, 1], F32, name="zero_column")
         nc.vector.memset(zero_column[:], 0.0)
@@ -56,7 +55,7 @@ def tile_scatter_matmul_kernel(tc, base, x, w, b, offs, out):
 
         window_tiles = [windows.tile([P, TOKENS], F32, name="window%d" % i) for i in range(SEQS)]
         for i in range(SEQS):
-            nc.tensor.matmul(window_tiles[i][:], ident[:], base_tiles[i][:], start=True, stop=False)
+            nc.tensor.matmul(window_tiles[i][:], ident[:], base_tile[:, i, :], start=True, stop=False)
 
         for i in range(SEQS):
             piece = offsets[:, i * PIECE_COLS : (i + 1) * PIECE_COLS]

import concourse.mybir as mybir
from concourse.masks import make_identity

BF16, F32, U16 = mybir.dt.bfloat16, mybir.dt.float32, mybir.dt.uint16
IDENTITY = mybir.ActivationFunctionType.Identity

P = 128
SEQS = 2
TOKENS = 512
HALF = TOKENS // 2
K = 512
KBLOCKS = K // P
N = 256
PIECE = N // SEQS
PIECE_COLS = PIECE // 16

WARMUP = 12

FLOPS = 2 * K * P * N


def tile_scatter_matmul_kernel(tc, base, x, w, b, offs, out):
    nc = tc.nc
    with (
        tc.tile_pool(name="held", bufs=1) as held,
        tc.psum_pool(name="windows", bufs=1) as windows,
    ):
        base_tile = held.tile([P, SEQS, TOKENS], BF16, name="base_tile")
        nc.sync.dma_start(base_tile[:], base.rearrange("i m t -> m i t"))

        offsets = held.tile([P, N // 16], U16, name="offsets")
        nc.sync.dma_start(offsets[:], offs)

        w_tile = held.tile([P, KBLOCKS, P], BF16, name="w_tile")
        nc.scalar.dma_start(w_tile[:], w.rearrange("(p a) m -> p a m", a=KBLOCKS))
        x_tile = held.tile([P, KBLOCKS, N], BF16, name="x_tile")
        nc.sync.dma_start(x_tile[:], x.rearrange("(p a) n -> p a n", a=KBLOCKS))

        bias = held.tile([P, 1], F32, name="bias")
        nc.gpsimd.dma_start(bias[:], b)

        ident = held.tile([P, P], BF16, name="ident")
        make_identity(nc, ident[:])

        zero_column = held.tile([P, 1], F32, name="zero_column")
        nc.vector.memset(zero_column[:], 0.0)
        unused_column = held.tile([P, 1], F32, name="unused_column")
        nc.scalar.activation(unused_column[:], zero_column[:], IDENTITY)

        zeros = held.tile([P, P], BF16, name="zeros")
        nc.vector.memset(zeros[:], 0.0)
        spare = windows.tile([P, P], F32, name="spare")
        for r in range(WARMUP):
            nc.tensor.matmul(spare[:], zeros[:], zeros[:], start=True, stop=True)

        window_tiles = [windows.tile([P, TOKENS], F32, name="window%d" % i) for i in range(SEQS)]
        for i in range(SEQS):
            nc.tensor.matmul(window_tiles[i][:], ident[:], base_tile[:, i, :], start=True, stop=False)

        for i in range(SEQS):
            piece = offsets[:, i * PIECE_COLS : (i + 1) * PIECE_COLS]
            for a in range(KBLOCKS):
                nc.tensor.matmul(
                    window_tiles[i][:].indirect(piece),
                    w_tile[:, a, :],
                    x_tile[:, a, i * PIECE : (i + 1) * PIECE],
                    start=False,
                    stop=(a == KBLOCKS - 1),
                )

        halves = [slice(h * HALF, (h + 1) * HALF) for h in range(2)]
        result_tiles = [
            [held.tile([P, HALF], F32, name="result%d_%d" % (i, h)) for h in range(2)] for i in range(SEQS)
        ]
        for h in range(2):
            nc.scalar.activation(
                result_tiles[0][h][:], window_tiles[0][:, halves[h]], IDENTITY, bias=bias[:, 0:1]
            )
        nc.sync.dma_start(out[0][:, halves[0]], result_tiles[0][0][:])
        nc.scalar.dma_start(out[0][:, halves[1]], result_tiles[0][1][:])
        for h in range(2):
            nc.vector.tensor_scalar_add(result_tiles[1][h][:], window_tiles[1][:, halves[h]], bias[:, 0:1])
            nc.sync.dma_start(out[1][:, halves[h]], result_tiles[1][h][:])
